import numpy as np, ml_dtypes
CORES = [144,200,272,328,400,456]
N = 6
KT, HT, TK = 4, 1, 128
def setup_inputs(rng):
    w = (rng.standard_normal((128, KT * HT * 128), dtype=np.float32) / 8).astype(ml_dtypes.bfloat16)
    return {"x": rng.standard_normal((N, 128, KT * TK), dtype=np.float32).astype(ml_dtypes.bfloat16), "w": np.broadcast_to(w, (N,) + w.shape).copy()}
def setup_inputs_big(rng):
    d = setup_inputs(rng)
    for k in ("x", "w"): d[k] = (d[k].astype(np.float32) * 1024.0).astype(d[k].dtype)
    return d
def setup_inputs_small(rng):
    d = setup_inputs(rng)
    for k in ("x", "w"): d[k] = (d[k].astype(np.float32) * (1 / 1024.0)).astype(d[k].dtype)
    return d
def setup_inputs_apart(rng):
    d = setup_inputs(rng)
    f = (10.0 ** rng.permutation(np.linspace(-1.5, 1.5, N))).astype(np.float32).reshape(N, 1, 1)
    for k in ("x",): d[k] = (d[k].astype(np.float32) * f).astype(d[k].dtype)
    return d
def tie_inputs(x):
    x = dict(x)
    x["w"] = np.broadcast_to(x["w"][0], x["w"].shape).copy()
    return x
def reference(x, w):
    X, W = x.astype(np.float64), w.astype(np.float64)
    def hidden(r):
        return np.stack([np.maximum(sum(W[r][:, 128 * (HT * t + u):128 * (HT * t + u) + 128].T @ X[r][:, TK * t:TK * t + TK] for t in range(KT)), 0.0) for u in range(HT)])
    h = [hidden(r) for r in range(N)]
    y = np.stack([sum(h[(r - 1) % N][u].T @ h[r][u] for u in range(HT)) for r in range(N)])
    return {"y": y.astype(ml_dtypes.bfloat16 if x.dtype != np.float64 else np.float64)}

@@ -1,0 +1,114 @@
+from concourse.mybir import AluOpType
+
+WORLD = 512
+KT = 4
+ENG_ON = 8
+ENG_OFF = 8
+
+SCRATCH = {
+    "xs": ("sbuf", [128, 512], "bfloat16"),
+    "ws": ("sbuf", [128, 512], "bfloat16"),
+    "zero": ("sbuf", [128, 128], "float32"),
+    "h": ("sbuf", [128, 128], "bfloat16"),
+    "hp": ("sbuf", [128, 128], "bfloat16"),
+    "ys": ("sbuf", [128, 128], "bfloat16"),
+    "ph": ("psum", [128, 512], "float32"),
+    "py": ("psum", [128, 512], "float32"),
+}
+SEMAPHORES = ["loaded", "zs", "mm", "hr", "arrived", "sent", "mm2", "yc", "stored"]
+
+
+def _same_chip(topo, a, b):
+    return topo.host(a) == topo.host(b) and topo.chip(a) == topo.chip(b)
+
+
+def _links(topo, a, b):
+    if _same_chip(topo, a, b):
+        return 0
+    if topo.rack(topo.host(a)) == topo.rack(topo.host(b)):
+        return 1 if (topo.mates(a, b) or topo.same_plane(a, b)) else 2
+    if topo.chip(a) == topo.chip(b):
+        return 1
+    twin = [c for c in range(WORLD) if topo.host(c) == topo.host(b) and topo.chip(c) == topo.chip(a)][0]
+    return 1 + _links(topo, twin, b)
+
+
+def _open_way(topo, a, b):
+    return int(topo.rack(topo.host(a)) != topo.rack(topo.host(b)) and topo.chip(a) != topo.chip(b))
+
+
+def _relay(topo, cores, s, d):
+    best = None
+    for c in range(WORLD):
+        if c in cores or not (topo.may_write(s, c) and topo.may_write(c, d)):
+            continue
+        key = ((not _same_chip(topo, s, c)) + (not _same_chip(topo, c, d)),
+               _links(topo, s, c) + _links(topo, c, d),
+               _open_way(topo, s, c) + _open_way(topo, c, d),
+               (topo.die(c) != topo.die(s)) + (topo.die(c) != topo.die(d)), c)
+        if best is None or key < best:
+            best = key
+    return best[-1]
+
+
+def _engines(topo, src, dst):
+    allowed = topo.mask(src, dst)
+    bits = [b for b in range(allowed.bit_length()) if (allowed >> b) & 1]
+    n = min(len(bits), ENG_ON if _same_chip(topo, src, dst) else ENG_OFF)
+    m = 0
+    for i in range(n):
+        m |= 1 << bits[i * len(bits) // n]
+    return m, n
+
+
+def _send(g, T, topo, src, dst, buf):
+    rid, pid = topo.addr(dst, src)
+    m, n = _engines(topo, src, dst)
+    g.remote_dma(out_ap=T.hp[:], in_ap=buf[:], remote_sem=T.sem.arrived, local_sem=T.sem.sent,
+                 pid=pid, routing_id=rid, dma_engine_mask=m)
+    return n
+
+
+def rank_program(g, core, T, topo):
+    cores = list(T.cores)
+    n_ranks = len(cores)
+    route = [(cores[r], _relay(topo, cores, cores[r], cores[(r + 1) % n_ranks]), cores[(r + 1) % n_ranks])
+             for r in range(n_ranks)]
+    rank = T.rank_of(core)
+
+    if rank is None:
+        for s, c, d in route:
+            if c == core:
+                g.wait_ge(T.sem.arrived, _engines(topo, s, c)[1])
+                n = _send(g, T, topo, c, d, T.hp)
+                g.wait_ge(T.sem.sent, n)
+        return
+
+    s, c, d = route[rank]
+    ps, pc, pd = route[(rank - 1) % n_ranks]
+
+    g.sync.dma_start(T.xs[:], T.x[:]).then_inc(T.sem.loaded, 16)
+    g.scalar.dma_start(T.ws[:], T.w[:]).then_inc(T.sem.loaded, 16)
+    g.vector.memset(T.zero[:], 0.0).then_inc(T.sem.zs, 1)
+    g.vector.wait_ge(T.sem.zs, 1)
+
+    g.tensor.wait_ge(T.sem.loaded, 32)
+    for t in range(KT):
+        mm = g.tensor.matmul(T.ph[:, 0:128], T.ws[:, 128 * t:128 * t + 128], T.xs[:, 128 * t:128 * t + 128],
+                             t == 0, t == KT - 1)
+    mm.then_inc(T.sem.mm, 1)
+    g.vector.wait_ge(T.sem.mm, 1)
+    g.vector.tensor_tensor(T.h[:], T.ph[:, 0:128], T.zero[:], AluOpType.max).then_inc(T.sem.hr, 1)
+
+    g.wait_ge(T.sem.hr, 1)
+    n = _send(g, T, topo, s, c, T.h)
+
+    g.tensor.wait_ge(T.sem.hr, 1)
+    g.tensor.wait_ge(T.sem.arrived, _engines(topo, pc, pd)[1])
+    g.tensor.matmul(T.py[:, 0:128], T.hp[:], T.h[:], True, True).then_inc(T.sem.mm2, 1)
+    g.vector.wait_ge(T.sem.mm2, 1)
+    g.vector.tensor_copy(T.ys[:], T.py[:, 0:128]).then_inc(T.sem.yc, 1)
+    g.sync.wait_ge(T.sem.yc, 1)
+    g.sync.dma_start(T.y[:], T.ys[:]).then_inc(T.sem.stored, 16)
+    g.sync.wait_ge(T.sem.stored, 16)
+    g.wait_ge(T.sem.sent, n)

@@ -2,20 +2,32 @@ from concourse.mybir import AluOpType
 
 WORLD = 512
 KT = 4
-ENG_ON = 8
-ENG_OFF = 8
+HC = 32
+LO = 128 - HC
+ENG_1 = 4
+ENG_2 = 8
 
 SCRATCH = {
     "xs": ("sbuf", [128, 512], "bfloat16"),
     "ws": ("sbuf", [128, 512], "bfloat16"),
-    "zero": ("sbuf", [128, 128], "float32"),
-    "h": ("sbuf", [128, 128], "bfloat16"),
+    "nw": ("sbuf", [128, 128], "bfloat16"),
+    "xo": ("sbuf", [128, HC], "bfloat16"),
+    "xh": ("sbuf", [128, HC], "bfloat16"),
+    "hb": ("sbuf", [128, 128], "bfloat16"),
     "hp": ("sbuf", [128, 128], "bfloat16"),
+    "h": ("sbuf", [128, 128], "bfloat16"),
+    "nh": ("sbuf", [128, 128], "bfloat16"),
+    "mb": ("sbuf", [128, HC], "bfloat16"),
     "ys": ("sbuf", [128, 128], "bfloat16"),
+    "yb": ("sbuf", [128, 128], "bfloat16"),
     "ph": ("psum", [128, 512], "float32"),
-    "py": ("psum", [128, 512], "float32"),
+    "ps": ("psum", [128, 512], "float32"),
+    "pq": ("psum", [128, 512], "float32"),
+    "pa": ("psum", [128, 512], "float32"),
+    "pb": ("psum", [128, 512], "float32"),
 }
-SEMAPHORES = ["loaded", "zs", "mm", "hr", "arrived", "sent", "mm2", "yc", "stored"]
+SEMAPHORES = ["lh", "loaded", "vn", "mms", "mm", "hbr", "hr", "ah", "ab", "sent", "mq", "vm", "ma", "mbs",
+              "ya", "yb", "st1", "st2"]
 
 
 def _same_chip(topo, a, b):
@@ -51,20 +63,20 @@ def _relay(topo, cores, s, d):
     return best[-1]
 
 
-def _engines(topo, src, dst):
+def _engines(topo, src, dst, want):
     allowed = topo.mask(src, dst)
     bits = [b for b in range(allowed.bit_length()) if (allowed >> b) & 1]
-    n = min(len(bits), ENG_ON if _same_chip(topo, src, dst) else ENG_OFF)
+    n = min(len(bits), want)
     m = 0
     for i in range(n):
         m |= 1 << bits[i * len(bits) // n]
     return m, n
 
 
-def _send(g, T, topo, src, dst, buf):
+def _send(g, T, topo, src, dst, want, out, buf, sem):
     rid, pid = topo.addr(dst, src)
-    m, n = _engines(topo, src, dst)
-    g.remote_dma(out_ap=T.hp[:], in_ap=buf[:], remote_sem=T.sem.arrived, local_sem=T.sem.sent,
+    m, n = _engines(topo, src, dst, want)
+    g.remote_dma(out_ap=out[:], in_ap=buf[:], remote_sem=sem, local_sem=T.sem.sent,
                  pid=pid, routing_id=rid, dma_engine_mask=m)
     return n
 
@@ -79,36 +91,71 @@ def rank_program(g, core, T, topo):
     if rank is None:
         for s, c, d in route:
             if c == core:
-                g.wait_ge(T.sem.arrived, _engines(topo, s, c)[1])
-                n = _send(g, T, topo, c, d, T.hp)
+                n1 = _engines(topo, s, c, ENG_1)[1]
+                g.wait_ge(T.sem.ah, n1)
+                n = _send(g, T, topo, c, d, ENG_2, T.xh, T.xh, T.sem.ah)
+                g.wait_ge(T.sem.ab, n1)
+                n += _send(g, T, topo, c, d, ENG_2, T.hp, T.hp, T.sem.ab)
                 g.wait_ge(T.sem.sent, n)
         return
 
     s, c, d = route[rank]
     ps, pc, pd = route[(rank - 1) % n_ranks]
+    n_in = _engines(topo, pc, pd, ENG_2)[1]
+    mx, mn, mul = AluOpType.max, AluOpType.min, AluOpType.mult
 
+    g.sync.dma_start(T.xo[:], T.x[:, LO:128]).then_inc(T.sem.lh, 16)
     g.sync.dma_start(T.xs[:], T.x[:]).then_inc(T.sem.loaded, 16)
     g.scalar.dma_start(T.ws[:], T.w[:]).then_inc(T.sem.loaded, 16)
-    g.vector.memset(T.zero[:], 0.0).then_inc(T.sem.zs, 1)
-    g.vector.wait_ge(T.sem.zs, 1)
+
+    g.wait_ge(T.sem.lh, 16)
+    n = _send(g, T, topo, s, c, ENG_1, T.xh, T.xo, T.sem.ah)
 
     g.tensor.wait_ge(T.sem.loaded, 32)
+    for t in range(1, KT):
+        mm = g.tensor.matmul(T.ps[:, 0:HC], T.ws[:, 128 * t:128 * t + 128], T.xs[:, 128 * t + LO:128 * t + 128],
+                             t == 1, t == KT - 1)
+    mm.then_inc(T.sem.mms, 1)
     for t in range(KT):
         mm = g.tensor.matmul(T.ph[:, 0:128], T.ws[:, 128 * t:128 * t + 128], T.xs[:, 128 * t:128 * t + 128],
                              t == 0, t == KT - 1)
     mm.then_inc(T.sem.mm, 1)
+
+    g.vector.wait_ge(T.sem.mms, 1)
+    g.vector.tensor_copy(T.hb[:, LO:128], T.ps[:, 0:HC]).then_inc(T.sem.hbr, 1)
     g.vector.wait_ge(T.sem.mm, 1)
-    g.vector.tensor_tensor(T.h[:], T.ph[:, 0:128], T.zero[:], AluOpType.max).then_inc(T.sem.hr, 1)
+    g.vector.tensor_scalar(T.hb[:, 0:LO], T.ph[:, 0:LO], 0.0, None, mx).then_inc(T.sem.hbr, 1)
+    g.vector.tensor_scalar(T.nw[:], T.ws[:, 0:128], -1.0, None, mul).then_inc(T.sem.vn, 1)
+    g.vector.tensor_scalar(T.h[:], T.ph[:, 0:128], 0.0, None, mx).then_inc(T.sem.hr, 1)
+    g.vector.tensor_scalar(T.nh[:], T.ph[:, 0:128], 0.0, -1.0, mx, mul).then_inc(T.sem.hr, 1)
 
-    g.wait_ge(T.sem.hr, 1)
-    n = _send(g, T, topo, s, c, T.h)
+    g.wait_ge(T.sem.hbr, 2)
+    n += _send(g, T, topo, s, c, ENG_1, T.hp, T.hb, T.sem.ab)
 
-    g.tensor.wait_ge(T.sem.hr, 1)
-    g.tensor.wait_ge(T.sem.arrived, _engines(topo, pc, pd)[1])
-    g.tensor.matmul(T.py[:, 0:128], T.hp[:], T.h[:], True, True).then_inc(T.sem.mm2, 1)
-    g.vector.wait_ge(T.sem.mm2, 1)
-    g.vector.tensor_copy(T.ys[:], T.py[:, 0:128]).then_inc(T.sem.yc, 1)
-    g.sync.wait_ge(T.sem.yc, 1)
-    g.sync.dma_start(T.y[:], T.ys[:]).then_inc(T.sem.stored, 16)
-    g.sync.wait_ge(T.sem.stored, 16)
+    g.tensor.wait_ge(T.sem.vn, 1)
+    g.tensor.wait_ge(T.sem.ah, n_in)
+    g.tensor.matmul(T.pq[:, 0:HC], T.nw[:], T.xh[:], True, True).then_inc(T.sem.mq, 1)
+
+    g.vector.wait_ge(T.sem.mq, 1)
+    g.vector.wait_ge(T.sem.ab, n_in)
+    g.vector.tensor_tensor(T.mb[:], T.pq[:, 0:HC], T.hp[:, LO:128], mn).then_inc(T.sem.vm, 1)
+
+    g.tensor.wait_ge(T.sem.hr, 2)
+    g.tensor.wait_ge(T.sem.ab, n_in)
+    g.tensor.matmul(T.pa[0:LO, 0:128], T.hp[:, 0:LO], T.h[:], True, True).then_inc(T.sem.ma, 1)
+    g.tensor.matmul(T.pb[0:HC, 0:128], T.hp[:, LO:128], T.h[:], True, False)
+    g.tensor.wait_ge(T.sem.vm, 1)
+    g.tensor.matmul(T.pb[0:HC, 0:128], T.mb[:], T.nh[:], False, True).then_inc(T.sem.mbs, 1)
+
+    g.vector.wait_ge(T.sem.ma, 1)
+    g.vector.tensor_copy(T.ys[0:LO, :], T.pa[0:LO, 0:128]).then_inc(T.sem.ya, 1)
+    g.vector.wait_ge(T.sem.mbs, 1)
+    g.vector.tensor_copy(T.yb[0:HC, :], T.pb[0:HC, 0:128]).then_inc(T.sem.yb, 1)
+
+    g.sync.wait_ge(T.sem.ya, 1)
+    g.sync.dma_start(T.y[0:LO, :], T.ys[0:LO, :]).then_inc(T.sem.st1, 16)
+    g.scalar.wait_ge(T.sem.yb, 1)
+    g.scalar.dma_start(T.y[LO:128, :], T.yb[0:HC, :]).then_inc(T.sem.st2, 16)
+    g.sync.wait_ge(T.sem.st1, 16)
+    g.scalar.wait_ge(T.sem.st2, 16)
     g.wait_ge(T.sem.sent, n)

from concourse.mybir import AluOpType

WORLD = 512
KT = 4
HC = 32
LO = 128 - HC
ENG_1 = 4
ENG_2 = 8

SCRATCH = {
    "xs": ("sbuf", [128, 512], "bfloat16"),
    "ws": ("sbuf", [128, 512], "bfloat16"),
    "nw": ("sbuf", [128, 128], "bfloat16"),
    "xo": ("sbuf", [128, HC], "bfloat16"),
    "xh": ("sbuf", [128, HC], "bfloat16"),
    "hb": ("sbuf", [128, 128], "bfloat16"),
    "hp": ("sbuf", [128, 128], "bfloat16"),
    "h": ("sbuf", [128, 128], "bfloat16"),
    "nh": ("sbuf", [128, 128], "bfloat16"),
    "mb": ("sbuf", [128, HC], "bfloat16"),
    "ys": ("sbuf", [128, 128], "bfloat16"),
    "yb": ("sbuf", [128, 128], "bfloat16"),
    "ph": ("psum", [128, 512], "float32"),
    "ps": ("psum", [128, 512], "float32"),
    "pq": ("psum", [128, 512], "float32"),
    "pa": ("psum", [128, 512], "float32"),
    "pb": ("psum", [128, 512], "float32"),
}
SEMAPHORES = ["lh", "loaded", "vn", "mms", "mm", "hbr", "hr", "ah", "ab", "sent", "mq", "vm", "ma", "mbs",
              "ya", "yb", "st1", "st2"]


def _same_chip(topo, a, b):
    return topo.host(a) == topo.host(b) and topo.chip(a) == topo.chip(b)


def _links(topo, a, b):
    if _same_chip(topo, a, b):
        return 0
    if topo.rack(topo.host(a)) == topo.rack(topo.host(b)):
        return 1 if (topo.mates(a, b) or topo.same_plane(a, b)) else 2
    if topo.chip(a) == topo.chip(b):
        return 1
    twin = [c for c in range(WORLD) if topo.host(c) == topo.host(b) and topo.chip(c) == topo.chip(a)][0]
    return 1 + _links(topo, twin, b)


def _open_way(topo, a, b):
    return int(topo.rack(topo.host(a)) != topo.rack(topo.host(b)) and topo.chip(a) != topo.chip(b))


def _relay(topo, cores, s, d):
    best = None
    for c in range(WORLD):
        if c in cores or not (topo.may_write(s, c) and topo.may_write(c, d)):
            continue
        key = ((not _same_chip(topo, s, c)) + (not _same_chip(topo, c, d)),
               _links(topo, s, c) + _links(topo, c, d),
               _open_way(topo, s, c) + _open_way(topo, c, d),
               (topo.die(c) != topo.die(s)) + (topo.die(c) != topo.die(d)), c)
        if best is None or key < best:
            best = key
    return best[-1]


def _engines(topo, src, dst, want):
    allowed = topo.mask(src, dst)
    bits = [b for b in range(allowed.bit_length()) if (allowed >> b) & 1]
    n = min(len(bits), want)
    m = 0
    for i in range(n):
        m |= 1 << bits[i * len(bits) // n]
    return m, n


def _send(g, T, topo, src, dst, want, out, buf, sem):
    rid, pid = topo.addr(dst, src)
    m, n = _engines(topo, src, dst, want)
    g.remote_dma(out_ap=out[:], in_ap=buf[:], remote_sem=sem, local_sem=T.sem.sent,
                 pid=pid, routing_id=rid, dma_engine_mask=m)
    return n


def rank_program(g, core, T, topo):
    cores = list(T.cores)
    n_ranks = len(cores)
    route = [(cores[r], _relay(topo, cores, cores[r], cores[(r + 1) % n_ranks]), cores[(r + 1) % n_ranks])
             for r in range(n_ranks)]
    rank = T.rank_of(core)

    if rank is None:
        for s, c, d in route:
            if c == core:
                n1 = _engines(topo, s, c, ENG_1)[1]
                g.wait_ge(T.sem.ah, n1)
                n = _send(g, T, topo, c, d, ENG_2, T.xh, T.xh, T.sem.ah)
                g.wait_ge(T.sem.ab, n1)
                n += _send(g, T, topo, c, d, ENG_2, T.hp, T.hp, T.sem.ab)
                g.wait_ge(T.sem.sent, n)
        return

    s, c, d = route[rank]
    ps, pc, pd = route[(rank - 1) % n_ranks]
    n_in = _engines(topo, pc, pd, ENG_2)[1]
    mx, mn, mul = AluOpType.max, AluOpType.min, AluOpType.mult

    g.sync.dma_start(T.xo[:], T.x[:, LO:128]).then_inc(T.sem.lh, 16)
    g.sync.dma_start(T.xs[:], T.x[:]).then_inc(T.sem.loaded, 16)
    g.scalar.dma_start(T.ws[:], T.w[:]).then_inc(T.sem.loaded, 16)

    g.wait_ge(T.sem.lh, 16)
    n = _send(g, T, topo, s, c, ENG_1, T.xh, T.xo, T.sem.ah)

    g.tensor.wait_ge(T.sem.loaded, 32)
    for t in range(1, KT):
        mm = g.tensor.matmul(T.ps[:, 0:HC], T.ws[:, 128 * t:128 * t + 128], T.xs[:, 128 * t + LO:128 * t + 128],
                             t == 1, t == KT - 1)
    mm.then_inc(T.sem.mms, 1)
    for t in range(KT):
        mm = g.tensor.matmul(T.ph[:, 0:128], T.ws[:, 128 * t:128 * t + 128], T.xs[:, 128 * t:128 * t + 128],
                             t == 0, t == KT - 1)
    mm.then_inc(T.sem.mm, 1)

    g.vector.wait_ge(T.sem.mms, 1)
    g.vector.tensor_copy(T.hb[:, LO:128], T.ps[:, 0:HC]).then_inc(T.sem.hbr, 1)
    g.vector.wait_ge(T.sem.mm, 1)
    g.vector.tensor_scalar(T.hb[:, 0:LO], T.ph[:, 0:LO], 0.0, None, mx).then_inc(T.sem.hbr, 1)
    g.vector.tensor_scalar(T.nw[:], T.ws[:, 0:128], -1.0, None, mul).then_inc(T.sem.vn, 1)
    g.vector.tensor_scalar(T.h[:], T.ph[:, 0:128], 0.0, None, mx).then_inc(T.sem.hr, 1)
    g.vector.tensor_scalar(T.nh[:], T.ph[:, 0:128], 0.0, -1.0, mx, mul).then_inc(T.sem.hr, 1)

    g.wait_ge(T.sem.hbr, 2)
    n += _send(g, T, topo, s, c, ENG_1, T.hp, T.hb, T.sem.ab)

    g.tensor.wait_ge(T.sem.vn, 1)
    g.tensor.wait_ge(T.sem.ah, n_in)
    g.tensor.matmul(T.pq[:, 0:HC], T.nw[:], T.xh[:], True, True).then_inc(T.sem.mq, 1)

    g.vector.wait_ge(T.sem.mq, 1)
    g.vector.wait_ge(T.sem.ab, n_in)
    g.vector.tensor_tensor(T.mb[:], T.pq[:, 0:HC], T.hp[:, LO:128], mn).then_inc(T.sem.vm, 1)

    g.tensor.wait_ge(T.sem.hr, 2)
    g.tensor.wait_ge(T.sem.ab, n_in)
    g.tensor.matmul(T.pa[0:LO, 0:128], T.hp[:, 0:LO], T.h[:], True, True).then_inc(T.sem.ma, 1)
    g.tensor.matmul(T.pb[0:HC, 0:128], T.hp[:, LO:128], T.h[:], True, False)
    g.tensor.wait_ge(T.sem.vm, 1)
    g.tensor.matmul(T.pb[0:HC, 0:128], T.mb[:], T.nh[:], False, True).then_inc(T.sem.mbs, 1)

    g.vector.wait_ge(T.sem.ma, 1)
    g.vector.tensor_copy(T.ys[0:LO, :], T.pa[0:LO, 0:128]).then_inc(T.sem.ya, 1)
    g.vector.wait_ge(T.sem.mbs, 1)
    g.vector.tensor_copy(T.yb[0:HC, :], T.pb[0:HC, 0:128]).then_inc(T.sem.yb, 1)

    g.sync.wait_ge(T.sem.ya, 1)
    g.sync.dma_start(T.y[0:LO, :], T.ys[0:LO, :]).then_inc(T.sem.st1, 16)
    g.scalar.wait_ge(T.sem.yb, 1)
    g.scalar.dma_start(T.y[LO:128, :], T.yb[0:HC, :]).then_inc(T.sem.st2, 16)
    g.sync.wait_ge(T.sem.st1, 16)
    g.scalar.wait_ge(T.sem.st2, 16)
    g.wait_ge(T.sem.sent, n)
